import numpy as np
import ml_dtypes


def mxq(x, axis, fmt="e4m3"):
    dtype, down = {"e4m3": (ml_dtypes.float8_e4m3fn, 7), "e5m2": (ml_dtypes.float8_e5m2, 14)}[fmt]
    v = np.moveaxis(np.asarray(x, np.float32).astype(ml_dtypes.bfloat16).astype(np.float64), axis, -1)
    blocks = v.reshape(v.shape[:-1] + (-1, 32))
    amax = np.abs(blocks).max(-1, keepdims=True)
    byte = np.maximum(np.where(amax > 0, np.frexp(amax)[1] - 1 + 127, 0) - down, 1)
    scale = np.exp2(byte - 127.0)
    codes = (blocks / scale).astype(np.float32).astype(dtype).astype(np.float64)
    return np.moveaxis((codes * scale).reshape(v.shape), -1, axis)


WIDE = False


def mx_kscale(k):
    if not WIDE:
        return np.ones(k)
    levels = np.array([10, -10, 5, -5, 0])
    if k % 512:
        return np.exp2(np.random.permutation(np.resize(levels, k // 32))).repeat(32)
    a = np.empty((k // 512, 16))
    for p in range(k // 512):
        a[p, :8] = np.random.permutation(np.resize(levels, 8))
        for g in range(8):
            far = levels[np.abs(levels - a[p, g]) >= 10]
            a[p, g + 8] = far[np.random.randint(len(far))]
    return np.exp2(a.ravel()).repeat(32)


def f64(x):
    return np.asarray(x).astype(np.float64)


def striped8(idx):
    return np.asarray(idx).reshape(8, -1, 16).transpose(0, 2, 1).reshape(128, -1).astype(np.uint16)


def unstriped8(offs):
    return offs.reshape(8, 16, -1).transpose(0, 2, 1).reshape(8, -1).astype(np.int64)


def pick8(x, idx, run):
    r = np.arange(len(x))
    return x[r[:, None], idx[r % (8 * run) // run]]


E2M1 = np.array([0.0, 0.5, 1.0, 1.5, 2.0, 3.0, 4.0, 6.0, -0.0, -0.5, -1.0, -1.5, -2.0, -3.0, -4.0, -6.0])


def pack_weight(w, fmt):
    k, n = w.shape
    w = f64(np.asarray(w, np.float32).astype(ml_dtypes.bfloat16)).reshape(k // 32, 32, n)
    amax = np.abs(w).max(1)
    if fmt == "e4m3":
        byte = np.frexp(amax)[1] - 1 + 127 - 7
    else:
        mant, ex = np.frexp(amax / 6.0)
        byte = np.where(mant > 0.5, ex, ex - 1) + 127
    byte = np.clip(np.where(amax > 0, byte, 1), 1, 254)
    scaled = (w * np.exp2(127.0 - byte)[:, None, :]).reshape(k, n).astype(np.float32)
    by_word = np.ascontiguousarray(scaled.reshape(k // 512, 128, 4, n).transpose(0, 1, 3, 2))
    if fmt == "e4m3":
        words = by_word.astype(ml_dtypes.float8_e4m3fn).view(np.uint8)
    else:
        c = by_word.astype(ml_dtypes.float4_e2m1fn).view(np.uint8) & 0xF
        words = (c[..., 0::2] | (c[..., 1::2] << 4)).reshape(k // 512, 128, 2 * n)
    return np.ascontiguousarray(words), np.ascontiguousarray(byte.astype(np.uint8).reshape(k // 512, 16, n))


def unpack_weight(words, scales, fmt):
    g, _, n = scales.shape
    words = np.ascontiguousarray(words).reshape(g, 128, n, -1)
    if fmt == "e4m3":
        vals = words.view(ml_dtypes.float8_e4m3fn).astype(np.float64)
    else:
        nib = np.empty((g, 128, n, 4), np.uint8)
        nib[..., 0::2] = words & 0xF
        nib[..., 1::2] = words >> 4
        vals = E2M1[nib]
    vals = vals * np.repeat(np.exp2(scales.astype(np.float64) - 127.0), 8, axis=1)[..., None]
    return vals.transpose(0, 1, 3, 2).reshape(g * 512, n)


D, T, U, Z, I, Q = 512, 1024, 1024, 1024, 512, 128


def setup_inputs():
    n = np.random.standard_normal
    idx = np.stack([np.random.permutation(T)[:I] for _ in range(8)])
    idx2 = np.stack([np.random.permutation(U)[:I] for _ in range(8)])
    idx3 = np.stack([np.random.permutation(Z)[:I] for _ in range(8)])
    idx4 = np.stack([np.random.permutation(T)[:I] for _ in range(8)])
    idx5 = np.stack([np.random.permutation(Z)[:I] for _ in range(8)])
    idx6 = np.stack([np.random.permutation(U)[:I] for _ in range(8)])
    fd = mx_kscale(D)
    keysp = pack_weight(n((D, T)) / fd[:, None], "e2m1")
    notesp = pack_weight(n((D, U)) / fd[:, None], "e4m3")
    return {
        "query": (n((D, Q)) * 1.0 / np.sqrt(D) * fd[:, None]).astype(np.float32),
        "keys_words": keysp[0],
        "keys_scales": keysp[1],
        "notes_words": notesp[0],
        "notes_scales": notesp[1],
        "lam": (np.random.uniform(0.5, 1.2, (Q, 1))).astype(np.float32),
        "offs": striped8(idx),
        "offs2": striped8(idx2),
        "offs3": striped8(idx3),
        "offs4": striped8(idx4),
        "offs5": striped8(idx5),
        "offs6": striped8(idx6),
    }


def reference(query, keys_words, keys_scales, notes_words, notes_scales, lam, offs, offs2, offs3, offs4, offs5, offs6):
    idx = unstriped8(offs)
    idx2 = unstriped8(offs2)
    idx3 = unstriped8(offs3)
    idx4 = unstriped8(offs4)
    idx5 = unstriped8(offs5)
    idx6 = unstriped8(offs6)
    keysu = unpack_weight(keys_words, keys_scales, "e2m1")
    notesu = unpack_weight(notes_words, notes_scales, "e4m3")
    queryq = mxq(f64(query), 0, "e4m3")
    a = queryq.T @ keysu
    b = queryq.T @ notesu
    w = pick8(a, idx, 16) - pick8(b, idx2, 16)
    f1 = np.zeros((Q, Z))
    f1[np.arange(Q)[:, None], idx3[np.arange(Q) % 128 // 16]] = w
    v = pick8(a, idx4, 16) + pick8(f1, idx5, 16)
    m1 = np.maximum(v, w)
    f2 = np.zeros((Q, U))
    f2[np.arange(Q)[:, None], idx2[np.arange(Q) % 128 // 16]] = m1
    bb = b + f2 * f64(lam)
    y = pick8(bb, idx6, 16)
    return y

@@ -1,0 +1,127 @@
+from contextlib import ExitStack
+
+import concourse.mybir as mybir
+
+F32 = mybir.dt.float32
+BF16 = mybir.dt.bfloat16
+I32 = mybir.dt.int32
+U32 = mybir.dt.uint32
+U16 = mybir.dt.uint16
+U8 = mybir.dt.uint8
+FP8X4 = mybir.dt.float8_e4m3fn_x4
+FP4X4 = mybir.dt.float4_e2m1fn_x4
+ALU = mybir.AluOpType
+COPY = mybir.ActivationFunctionType.Copy
+
+P = 128
+D, T, SLOTS, Q = 512, 1024, 512, 128
+HALF = SLOTS // 2
+FLOPS = 2 * D * Q * 2 * T
+
+
+def tile_attend_stakes_two_kernel(tc, query, keys_words, keys_scales, notes_words, notes_scales, lam,
+                                   offs, offs2, offs3, offs4, offs5, offs6, out):
+    nc = tc.nc
+    with ExitStack() as ctx:
+        sb = ctx.enter_context(tc.tile_pool(name="sb", bufs=1))
+        ps = ctx.enter_context(tc.psum_pool(name="ps", bufs=1))
+
+        def f32(name, width):
+            return sb.tile([P, width], F32, name=name, align_bytes=64)
+
+        def load_list(name, src):
+            t = sb.tile([P, SLOTS // 16], U16, name=name)
+            nc.sync.dma_start(t[:], src)
+            return t
+
+        def load_scales(t, src):
+            for r in range(4):
+                nc.sync.dma_start(t[:].bitcast(I32)[r:P:32, :], src[0].bitcast(I32)[r:16:4, :])
+
+        def half(lst, h):
+            return lst[:, h * HALF // 16:(h + 1) * HALF // 16]
+
+        n_sc = sb.tile([P, T], U8, name="n_sc", align_bytes=64)
+        k_sc = sb.tile([P, T], U8, name="k_sc", align_bytes=64)
+        nc.vector.memset(n_sc[:].bitcast(I32), 0)
+        nc.vector.memset(k_sc[:].bitcast(I32), 0)
+
+        q_raw = sb.tile([P, 4, Q], F32, name="q_raw")
+        nc.sync.dma_start(q_raw[:], query.rearrange("(p j) w -> p j w", j=4))
+        l2 = load_list("l2", offs2)
+        load_scales(n_sc, notes_scales)
+        n_w = sb.tile([P, T], U32, name="n_w", align_bytes=64)
+        nc.sync.dma_start(n_w[:].bitcast(I32), notes_words[0].rearrange("p n t -> p (n t)").bitcast(I32))
+        k_w = sb.tile([P, 2 * T], U8, name="k_w", align_bytes=64)
+        nc.sync.dma_start(k_w[:].bitcast(I32), keys_words[0].bitcast(I32))
+        load_scales(k_sc, keys_scales)
+        l1 = load_list("l1", offs)
+        l3 = load_list("l3", offs3)
+        l4 = load_list("l4", offs4)
+        l5 = load_list("l5", offs5)
+        l6 = load_list("l6", offs6)
+        lam_t = sb.tile([P, 1], F32, name="lam_t")
+        nc.sync.dma_start(lam_t[:], lam)
+
+        f1 = f32("f1", T)
+        f2 = f32("f2", T)
+        nc.vector.memset(f1[:], 0.0)
+        nc.vector.memset(f2[:], 0.0)
+
+        q_bf = sb.tile([P, Q, 4], BF16, name="q_bf", align_bytes=64)
+        nc.vector.tensor_copy(q_bf[:], q_raw[:].rearrange("p j w -> p w j"))
+        q_w = sb.tile([P, Q], U32, name="q_w", align_bytes=64)
+        q_sc = sb.tile([P, Q], U8, name="q_sc", align_bytes=64)
+        nc.vector.quantize_mx(out=q_w[:].bitcast(FP8X4), scales=q_sc[:], in_=q_bf[:].rearrange("p w j -> p (w j)"))
+
+        a = f32("a", T)
+        b = f32("b", T)
+
+        def score(dst, name, c0, c1, rhs, sc, on_scalar):
+            acc = ps.tile([P, c1 - c0], F32, name=name)
+            nc.tensor.matmul_mx(out=acc[:], lhsT=q_w[:].bitcast(FP8X4), lhsT_scale=q_sc[:], rhs=rhs,
+                                rhs_scale=sc[:, c0:c1], start=True, stop=True)
+            if on_scalar:
+                nc.scalar.activation(dst[:, c0:c1], acc[:], COPY)
+            else:
+                nc.vector.tensor_copy(dst[:, c0:c1], acc[:])
+
+        for c0, c1, s in ((0, 256, True), (256, 512, False), (512, 768, True), (768, 1024, False)):
+            score(b, "pb%d" % c0, c0, c1, n_w[:, c0:c1].bitcast(FP8X4), n_sc, s)
+        gb = [f32("gb0", HALF), f32("ngb1", HALF)]
+        nc.scalar.activation(gb[0][:], b[:].indirect(half(l2, 0)), COPY)
+        for c0, c1, s in ((0, 256, False), (256, 512, False), (512, 768, False), (768, 1024, False)):
+            score(a, "pa%d" % c0, c0, c1, k_w[:, 2 * c0:2 * c1].bitcast(FP4X4), k_sc, s)
+
+        w = [f32("w0", HALF), f32("w1", HALF)]
+        nc.vector.tensor_tensor(w[0][:], a[:].indirect(half(l1, 0)), gb[0][:], ALU.subtract)
+        ga1 = f32("ga1", HALF)
+        nc.scalar.activation(gb[1][:], b[:].indirect(half(l2, 1)), COPY, scale=-1.0)
+        nc.scalar.activation(ga1[:], a[:].indirect(half(l1, 1)), COPY)
+        ga4 = [f32("ga40", HALF), f32("ga41", HALF)]
+        for h in range(2):
+            nc.scalar.activation(ga4[h][:], a[:].indirect(half(l4, h)), COPY)
+
+        nc.vector.tensor_copy(f1[:].indirect(half(l3, 0)), w[0][:])
+        nc.vector.tensor_tensor(f1[:].indirect(half(l3, 1)), ga1[:], gb[1][:], ALU.add)
+        nc.vector.tensor_tensor(w[1][:], ga1[:], gb[1][:], ALU.add)
+
+        v = [f32("v0", HALF), f32("v1", HALF)]
+        gf1 = f32("gf1", HALF)
+        nc.vector.tensor_tensor(v[0][:], f1[:].indirect(half(l5, 0)), ga4[0][:], ALU.add)
+        nc.scalar.activation(gf1[:], f1[:].indirect(half(l5, 1)), COPY)
+        nc.vector.tensor_tensor(v[1][:], gf1[:], ga4[1][:], ALU.add)
+        m = [f32("m0", HALF), f32("m1", HALF)]
+        for h in range(2):
+            nc.vector.tensor_tensor(m[h][:], v[h][:], w[h][:], ALU.max)
+        for h in range(2):
+            nc.vector.tensor_copy(f2[:].indirect(half(l2, h)), m[h][:])
+
+        bb = f32("bb", T)
+        nc.vector.scalar_tensor_tensor(bb[:], f2[:], lam_t[:], b[:], ALU.mult, ALU.add)
+
+        y = [f32("y0", HALF), f32("y1", HALF)]
+        nc.vector.tensor_copy(y[0][:], bb[:].indirect(half(l6, 0)))
+        nc.scalar.activation(y[1][:], bb[:].indirect(half(l6, 1)), COPY)
+        nc.sync.dma_start(out[:, 0:HALF], y[0][:])
+        nc.scalar.dma_start(out[:, HALF:SLOTS], y[1][:])

@@ -43,19 +43,21 @@ def tile_attend_stakes_two_kernel(tc, query, keys_words, keys_scales, notes_word
 
         n_sc = sb.tile([P, T], U8, name="n_sc", align_bytes=64)
         k_sc = sb.tile([P, T], U8, name="k_sc", align_bytes=64)
-        nc.vector.memset(n_sc[:].bitcast(I32), 0)
         nc.vector.memset(k_sc[:].bitcast(I32), 0)
+        nc.vector.memset(n_sc[:].bitcast(I32), 0)
 
         q_raw = sb.tile([P, 4, Q], F32, name="q_raw")
         nc.sync.dma_start(q_raw[:], query.rearrange("(p j) w -> p j w", j=4))
-        l2 = load_list("l2", offs2)
-        load_scales(n_sc, notes_scales)
-        n_w = sb.tile([P, T], U32, name="n_w", align_bytes=64)
-        nc.sync.dma_start(n_w[:].bitcast(I32), notes_words[0].rearrange("p n t -> p (n t)").bitcast(I32))
+        load_scales(k_sc, keys_scales)
         k_w = sb.tile([P, 2 * T], U8, name="k_w", align_bytes=64)
         nc.sync.dma_start(k_w[:].bitcast(I32), keys_words[0].bitcast(I32))
-        load_scales(k_sc, keys_scales)
+        n_w = [sb.tile([P, T // 2], U32, name="n_w%d" % h, align_bytes=64) for h in range(2)]
+        n_src = notes_words[0].rearrange("p n t -> p (n t)").bitcast(I32)
+        for h in range(2):
+            nc.sync.dma_start(n_w[h][:].bitcast(I32), n_src[:, h * T // 2:(h + 1) * T // 2])
+        load_scales(n_sc, notes_scales)
         l1 = load_list("l1", offs)
+        l2 = load_list("l2", offs2)
         l3 = load_list("l3", offs3)
         l4 = load_list("l4", offs4)
         l5 = load_list("l5", offs5)
@@ -68,11 +70,15 @@ def tile_attend_stakes_two_kernel(tc, query, keys_words, keys_scales, notes_word
         nc.vector.memset(f1[:], 0.0)
         nc.vector.memset(f2[:], 0.0)
 
-        q_bf = sb.tile([P, Q, 4], BF16, name="q_bf", align_bytes=64)
-        nc.vector.tensor_copy(q_bf[:], q_raw[:].rearrange("p j w -> p w j"))
         q_w = sb.tile([P, Q], U32, name="q_w", align_bytes=64)
         q_sc = sb.tile([P, Q], U8, name="q_sc", align_bytes=64)
-        nc.vector.quantize_mx(out=q_w[:].bitcast(FP8X4), scales=q_sc[:], in_=q_bf[:].rearrange("p w j -> p (w j)"))
+        q_bf = [sb.tile([P, Q // 2, 4], BF16, name="q_bf%d" % h, align_bytes=64) for h in range(2)]
+        for h in range(2):
+            nc.vector.tensor_copy(q_bf[h][:], q_raw[:, :, h * Q // 2:(h + 1) * Q // 2].rearrange("p j w -> p w j"))
+        for h in range(2):
+            cols = slice(h * Q // 2, (h + 1) * Q // 2)
+            nc.vector.quantize_mx(out=q_w[:, cols].bitcast(FP8X4), scales=q_sc[:, cols],
+                                  in_=q_bf[h][:].rearrange("p w j -> p (w j)"))
 
         a = f32("a", T)
         b = f32("b", T)
@@ -87,35 +93,35 @@ def tile_attend_stakes_two_kernel(tc, query, keys_words, keys_scales, notes_word
                 nc.vector.tensor_copy(dst[:, c0:c1], acc[:])
 
         for c0, c1, s in ((0, 256, True), (256, 512, False), (512, 768, True), (768, 1024, False)):
-            score(b, "pb%d" % c0, c0, c1, n_w[:, c0:c1].bitcast(FP8X4), n_sc, s)
-        gb = [f32("gb0", HALF), f32("ngb1", HALF)]
-        nc.scalar.activation(gb[0][:], b[:].indirect(half(l2, 0)), COPY)
-        for c0, c1, s in ((0, 256, False), (256, 512, False), (512, 768, False), (768, 1024, False)):
             score(a, "pa%d" % c0, c0, c1, k_w[:, 2 * c0:2 * c1].bitcast(FP4X4), k_sc, s)
+        ga = [f32("ga0", HALF), f32("ga1", HALF)]
+        for h in range(2):
+            nc.scalar.activation(ga[h][:], a[:].indirect(half(l1, h)), COPY)
+        for c0, c1, s in ((0, 256, False), (256, 512, False), (512, 768, False), (768, 1024, False)):
+            score(b, "pb%d" % c0, c0, c1, n_w[c0 // 512][:, c0 % 512:c0 % 512 + c1 - c0].bitcast(FP8X4), n_sc, s)
 
-        w = [f32("w0", HALF), f32("w1", HALF)]
-        nc.vector.tensor_tensor(w[0][:], a[:].indirect(half(l1, 0)), gb[0][:], ALU.subtract)
-        ga1 = f32("ga1", HALF)
-        nc.scalar.activation(gb[1][:], b[:].indirect(half(l2, 1)), COPY, scale=-1.0)
-        nc.scalar.activation(ga1[:], a[:].indirect(half(l1, 1)), COPY)
+        ngb = [f32("ngb0", HALF), f32("ngb1", HALF)]
+        nc.vector.tensor_scalar(ngb[0][:], b[:].indirect(half(l2, 0)), -1.0, 0.0, ALU.mult, ALU.add)
+        nc.scalar.activation(ngb[1][:], b[:].indirect(half(l2, 1)), COPY, scale=-1.0)
         ga4 = [f32("ga40", HALF), f32("ga41", HALF)]
         for h in range(2):
             nc.scalar.activation(ga4[h][:], a[:].indirect(half(l4, h)), COPY)
 
-        nc.vector.tensor_copy(f1[:].indirect(half(l3, 0)), w[0][:])
-        nc.vector.tensor_tensor(f1[:].indirect(half(l3, 1)), ga1[:], gb[1][:], ALU.add)
-        nc.vector.tensor_tensor(w[1][:], ga1[:], gb[1][:], ALU.add)
+        w = [f32("w0", HALF), ngb[0]]
+        for h in range(2):
+            nc.vector.tensor_tensor(f1[:].indirect(half(l3, h)), ga[h][:], ngb[h][:], ALU.add)
+        for h in range(2):
+            nc.vector.tensor_tensor(w[h][:], ga[h][:], ngb[h][:], ALU.add)
 
         v = [f32("v0", HALF), f32("v1", HALF)]
         gf1 = f32("gf1", HALF)
         nc.vector.tensor_tensor(v[0][:], f1[:].indirect(half(l5, 0)), ga4[0][:], ALU.add)
         nc.scalar.activation(gf1[:], f1[:].indirect(half(l5, 1)), COPY)
         nc.vector.tensor_tensor(v[1][:], gf1[:], ga4[1][:], ALU.add)
-        m = [f32("m0", HALF), f32("m1", HALF)]
+        m = sb.tile([P, SLOTS], F32, name="m", tag="f1", align_bytes=64)
         for h in range(2):
-            nc.vector.tensor_tensor(m[h][:], v[h][:], w[h][:], ALU.max)
-        for h in range(2):
-            nc.vector.tensor_copy(f2[:].indirect(half(l2, h)), m[h][:])
+            nc.vector.tensor_tensor(m[:, h * HALF:(h + 1) * HALF], v[h][:], w[h][:], ALU.max)
+        nc.vector.tensor_copy(f2[:].indirect(l2[:]), m[:])
 
         bb = f32("bb", T)
         nc.vector.scalar_tensor_tensor(bb[:], f2[:], lam_t[:], b[:], ALU.mult, ALU.add)

from contextlib import ExitStack

import concourse.mybir as mybir

F32 = mybir.dt.float32
BF16 = mybir.dt.bfloat16
I32 = mybir.dt.int32
U32 = mybir.dt.uint32
U16 = mybir.dt.uint16
U8 = mybir.dt.uint8
FP8X4 = mybir.dt.float8_e4m3fn_x4
FP4X4 = mybir.dt.float4_e2m1fn_x4
ALU = mybir.AluOpType
COPY = mybir.ActivationFunctionType.Copy

P = 128
D, T, SLOTS, Q = 512, 1024, 512, 128
HALF = SLOTS // 2
FLOPS = 2 * D * Q * 2 * T


def tile_attend_stakes_two_kernel(tc, query, keys_words, keys_scales, notes_words, notes_scales, lam,
                                   offs, offs2, offs3, offs4, offs5, offs6, out):
    nc = tc.nc
    with ExitStack() as ctx:
        sb = ctx.enter_context(tc.tile_pool(name="sb", bufs=1))
        ps = ctx.enter_context(tc.psum_pool(name="ps", bufs=1))

        def f32(name, width):
            return sb.tile([P, width], F32, name=name, align_bytes=64)

        def load_list(name, src):
            t = sb.tile([P, SLOTS // 16], U16, name=name)
            nc.sync.dma_start(t[:], src)
            return t

        def load_scales(t, src):
            for r in range(4):
                nc.sync.dma_start(t[:].bitcast(I32)[r:P:32, :], src[0].bitcast(I32)[r:16:4, :])

        def half(lst, h):
            return lst[:, h * HALF // 16:(h + 1) * HALF // 16]

        n_sc = sb.tile([P, T], U8, name="n_sc", align_bytes=64)
        k_sc = sb.tile([P, T], U8, name="k_sc", align_bytes=64)
        nc.vector.memset(k_sc[:].bitcast(I32), 0)
        nc.vector.memset(n_sc[:].bitcast(I32), 0)

        q_raw = sb.tile([P, 4, Q], F32, name="q_raw")
        nc.sync.dma_start(q_raw[:], query.rearrange("(p j) w -> p j w", j=4))
        load_scales(k_sc, keys_scales)
        k_w = sb.tile([P, 2 * T], U8, name="k_w", align_bytes=64)
        nc.sync.dma_start(k_w[:].bitcast(I32), keys_words[0].bitcast(I32))
        n_w = [sb.tile([P, T // 2], U32, name="n_w%d" % h, align_bytes=64) for h in range(2)]
        n_src = notes_words[0].rearrange("p n t -> p (n t)").bitcast(I32)
        for h in range(2):
            nc.sync.dma_start(n_w[h][:].bitcast(I32), n_src[:, h * T // 2:(h + 1) * T // 2])
        load_scales(n_sc, notes_scales)
        l1 = load_list("l1", offs)
        l2 = load_list("l2", offs2)
        l3 = load_list("l3", offs3)
        l4 = load_list("l4", offs4)
        l5 = load_list("l5", offs5)
        l6 = load_list("l6", offs6)
        lam_t = sb.tile([P, 1], F32, name="lam_t")
        nc.sync.dma_start(lam_t[:], lam)

        f1 = f32("f1", T)
        f2 = f32("f2", T)
        nc.vector.memset(f1[:], 0.0)
        nc.vector.memset(f2[:], 0.0)

        q_w = sb.tile([P, Q], U32, name="q_w", align_bytes=64)
        q_sc = sb.tile([P, Q], U8, name="q_sc", align_bytes=64)
        q_bf = [sb.tile([P, Q // 2, 4], BF16, name="q_bf%d" % h, align_bytes=64) for h in range(2)]
        for h in range(2):
            nc.vector.tensor_copy(q_bf[h][:], q_raw[:, :, h * Q // 2:(h + 1) * Q // 2].rearrange("p j w -> p w j"))
        for h in range(2):
            cols = slice(h * Q // 2, (h + 1) * Q // 2)
            nc.vector.quantize_mx(out=q_w[:, cols].bitcast(FP8X4), scales=q_sc[:, cols],
                                  in_=q_bf[h][:].rearrange("p w j -> p (w j)"))

        a = f32("a", T)
        b = f32("b", T)

        def score(dst, name, c0, c1, rhs, sc, on_scalar):
            acc = ps.tile([P, c1 - c0], F32, name=name)
            nc.tensor.matmul_mx(out=acc[:], lhsT=q_w[:].bitcast(FP8X4), lhsT_scale=q_sc[:], rhs=rhs,
                                rhs_scale=sc[:, c0:c1], start=True, stop=True)
            if on_scalar:
                nc.scalar.activation(dst[:, c0:c1], acc[:], COPY)
            else:
                nc.vector.tensor_copy(dst[:, c0:c1], acc[:])

        for c0, c1, s in ((0, 256, True), (256, 512, False), (512, 768, True), (768, 1024, False)):
            score(a, "pa%d" % c0, c0, c1, k_w[:, 2 * c0:2 * c1].bitcast(FP4X4), k_sc, s)
        ga = [f32("ga0", HALF), f32("ga1", HALF)]
        for h in range(2):
            nc.scalar.activation(ga[h][:], a[:].indirect(half(l1, h)), COPY)
        for c0, c1, s in ((0, 256, False), (256, 512, False), (512, 768, False), (768, 1024, False)):
            score(b, "pb%d" % c0, c0, c1, n_w[c0 // 512][:, c0 % 512:c0 % 512 + c1 - c0].bitcast(FP8X4), n_sc, s)

        ngb = [f32("ngb0", HALF), f32("ngb1", HALF)]
        nc.vector.tensor_scalar(ngb[0][:], b[:].indirect(half(l2, 0)), -1.0, 0.0, ALU.mult, ALU.add)
        nc.scalar.activation(ngb[1][:], b[:].indirect(half(l2, 1)), COPY, scale=-1.0)
        ga4 = [f32("ga40", HALF), f32("ga41", HALF)]
        for h in range(2):
            nc.scalar.activation(ga4[h][:], a[:].indirect(half(l4, h)), COPY)

        w = [f32("w0", HALF), ngb[0]]
        for h in range(2):
            nc.vector.tensor_tensor(f1[:].indirect(half(l3, h)), ga[h][:], ngb[h][:], ALU.add)
        for h in range(2):
            nc.vector.tensor_tensor(w[h][:], ga[h][:], ngb[h][:], ALU.add)

        v = [f32("v0", HALF), f32("v1", HALF)]
        gf1 = f32("gf1", HALF)
        nc.vector.tensor_tensor(v[0][:], f1[:].indirect(half(l5, 0)), ga4[0][:], ALU.add)
        nc.scalar.activation(gf1[:], f1[:].indirect(half(l5, 1)), COPY)
        nc.vector.tensor_tensor(v[1][:], gf1[:], ga4[1][:], ALU.add)
        m = sb.tile([P, SLOTS], F32, name="m", tag="f1", align_bytes=64)
        for h in range(2):
            nc.vector.tensor_tensor(m[:, h * HALF:(h + 1) * HALF], v[h][:], w[h][:], ALU.max)
        nc.vector.tensor_copy(f2[:].indirect(l2[:]), m[:])

        bb = f32("bb", T)
        nc.vector.scalar_tensor_tensor(bb[:], f2[:], lam_t[:], b[:], ALU.mult, ALU.add)

        y = [f32("y0", HALF), f32("y1", HALF)]
        nc.vector.tensor_copy(y[0][:], bb[:].indirect(half(l6, 0)))
        nc.scalar.activation(y[1][:], bb[:].indirect(half(l6, 1)), COPY)
        nc.sync.dma_start(out[:, 0:HALF], y[0][:])
        nc.scalar.dma_start(out[:, HALF:SLOTS], y[1][:])
